import numpy as np
import ml_dtypes


def mxq(x, axis, fmt="e4m3"):
    dtype, down = {"e4m3": (ml_dtypes.float8_e4m3fn, 7), "e5m2": (ml_dtypes.float8_e5m2, 14)}[fmt]
    v = np.moveaxis(np.asarray(x, np.float32).astype(ml_dtypes.bfloat16).astype(np.float64), axis, -1)
    blocks = v.reshape(v.shape[:-1] + (-1, 32))
    amax = np.abs(blocks).max(-1, keepdims=True)
    byte = np.maximum(np.where(amax > 0, np.frexp(amax)[1] - 1 + 127, 0) - down, 1)
    scale = np.exp2(byte - 127.0)
    codes = (blocks / scale).astype(np.float32).astype(dtype).astype(np.float64)
    return np.moveaxis((codes * scale).reshape(v.shape), -1, axis)


WIDE = False


def mx_kscale(k):
    if not WIDE:
        return np.ones(k)
    levels = np.array([10, -10, 5, -5, 0])
    if k % 512:
        return np.exp2(np.random.permutation(np.resize(levels, k // 32))).repeat(32)
    a = np.empty((k // 512, 16))
    for p in range(k // 512):
        a[p, :8] = np.random.permutation(np.resize(levels, 8))
        for g in range(8):
            far = levels[np.abs(levels - a[p, g]) >= 10]
            a[p, g + 8] = far[np.random.randint(len(far))]
    return np.exp2(a.ravel()).repeat(32)


def f64(x):
    return np.asarray(x).astype(np.float64)


def striped(idx):
    return np.tile(idx.reshape(-1, 16).T, (8, 1)).astype(np.uint16)


def unstriped(offs):
    return offs[:16].T.reshape(-1).astype(np.int64)


def pack_weight(w):
    k, n = w.shape
    w = f64(np.asarray(w, np.float32).astype(ml_dtypes.bfloat16)).reshape(k // 32, 32, n)
    amax = np.abs(w).max(1)
    byte = np.clip(np.where(amax > 0, np.frexp(amax)[1] - 1 + 127 - 7, 1), 1, 254)
    scaled = (w * np.exp2(127.0 - byte)[:, None, :]).reshape(k, n).astype(np.float32)
    words = np.ascontiguousarray(scaled.reshape(k // 512, 128, 4, n).transpose(0, 1, 3, 2)).astype(ml_dtypes.float8_e4m3fn).view(np.uint8)
    return words, np.ascontiguousarray(byte.astype(np.uint8).reshape(k // 512, 16, n))


def unpack_weight(words, scales):
    g, p, n, _ = words.shape
    vals = np.ascontiguousarray(words).view(ml_dtypes.float8_e4m3fn).astype(np.float64) * np.repeat(np.exp2(scales.astype(np.float64) - 127.0), 8, axis=1)[..., None]
    return vals.transpose(0, 1, 3, 2).reshape(g * 512, n)


def relu(v):
    return np.maximum(v, 0.0)


K, T, S, D, N, H = 512, 2048, 512, 4, 128, 512


def setup_inputs():
    n = np.random.standard_normal
    s = mx_kscale(K)[:, None]
    u = mx_kscale(H)
    packed_xT = pack_weight(n((K, T)) * s)
    return {
        "x_words": packed_xT[0],
        "x_scales": packed_xT[1],
        "w1": (n((K, H)) / np.sqrt(K) / s).astype(np.float32),
        "w2": (n((K, H)) / np.sqrt(K) / s).astype(np.float32),
        "cost": (np.random.uniform(0.0, 1.5, (H, S))).astype(np.float32),
        "unit": (np.random.uniform(0.6, 1.4, (H, 1)) * u[:, None]).astype(np.float32),
        "w3": (n((H, N)) / np.sqrt(H) / u[:, None]).astype(np.float32),
        "offs": striped(np.random.permutation(T)[:S]),
        "blk": striped(np.random.permutation(S)),
    }


def reference(x_words, x_scales, w1, w2, cost, unit, w3, offs, blk):
    xq = unpack_weight(x_words, x_scales)[:, unstriped(offs)]
    du = mxq(f64(w2), 0, "e4m3").T @ xq
    y = mxq(f64(w1), 0, "e4m3").T @ xq
    rc = f64(cost) - np.tanh(y)
    best = rc.reshape(len(rc), -1, D).min(axis=2)
    enter = relu(-1.0 * (np.repeat(best, D, axis=1) + rc))
    adu = np.abs(du)
    ab = adu[:, unstriped(blk)]
    step = enter / (ab + 0.4)
    sb = step[:, unstriped(blk)]
    newd = du + sb - (0.5 * step)
    hid = f64(unit) * newd
    return mxq(f64(w3), 0, "e4m3").T @ mxq(hid, 0, "e4m3")

@@ -1,0 +1,168 @@
+from contextlib import ExitStack
+
+import concourse.mybir as mybir
+
+K, T, S, D, N, H = 512, 2048, 512, 4, 128, 512
+FLOPS = 2 * K * H * S * 2 + 2 * H * N * S
+
+F32 = mybir.dt.float32
+BF16 = mybir.dt.bfloat16
+I32 = mybir.dt.int32
+U32 = mybir.dt.uint32
+U16 = mybir.dt.uint16
+U8 = mybir.dt.uint8
+FP8X4 = mybir.dt.float8_e4m3fn_x4
+ALU = mybir.AluOpType
+ACT = mybir.ActivationFunctionType
+
+P = 128
+PACK = 4
+V_SHARE = 80
+HALF = S // 2
+SCALAR_FETCH = 2
+
+
+def tile_picked_ybender_dual_p_kernel(tc, x_words, x_scales, w1, w2, cost, unit, w3, offs, blk, out):
+    nc = tc.nc
+    with ExitStack() as ctx:
+        keep = ctx.enter_context(tc.tile_pool(name="keep", bufs=1))
+        psum = ctx.enter_context(tc.psum_pool(name="psum", bufs=4))
+
+        offs_sb = keep.tile([P, S // 16], U16, name="offs_sb")
+        blk_sb = keep.tile([P, S // 16], U16, name="blk_sb")
+        xw = keep.tile([P, T], U32, name="xw")
+        xs = keep.tile([P, T], U8, name="xs")
+        w1_raw = keep.tile([P, PACK, H], F32, name="w1_raw")
+        w2_raw = keep.tile([P, PACK, H], F32, name="w2_raw")
+        w3_raw = keep.tile([P, PACK, N], F32, name="w3_raw")
+        cost_sb = [keep.tile([P, S], F32, name="cost%d" % t) for t in range(PACK)]
+        unit_sb = keep.tile([P, PACK], F32, name="unit_sb")
+
+        nc.gpsimd.memset(xs[:].bitcast(I32), 0)
+        nc.sync.dma_start(offs_sb[:], offs)
+        nc.sync.dma_start(xw[:].bitcast(I32), x_words[0].rearrange("p n t -> p (n t)").bitcast(I32))
+        for q in range(4):
+            nc.sync.dma_start(xs[32 * q : 32 * q + 4, :].bitcast(I32), x_scales[0, 4 * q : 4 * q + 4, :].bitcast(I32))
+        nc.sync.dma_start(w1_raw[:], w1.rearrange("(p j) c -> p j c", j=PACK))
+        nc.sync.dma_start(w2_raw[:], w2.rearrange("(p j) c -> p j c", j=PACK))
+        cost_v = cost.rearrange("(p t) s -> p t s", t=PACK)
+        nc.sync.dma_start(unit_sb[:], unit.rearrange("(p t) o -> p (t o)", t=PACK))
+        for t in range(PACK):
+            nc.sync.dma_start(cost_sb[t][:], cost_v[:, t, :])
+        nc.sync.dma_start(blk_sb[:], blk)
+        nc.sync.dma_start(w3_raw[:], w3.rearrange("(p j) c -> p j c", j=PACK))
+
+        xw_g = keep.tile([P, S], U32, name="xw_g", align_bytes=64)
+        xs_g = keep.tile([P, S], U8, name="xs_g", align_bytes=64)
+        nc.vector.tensor_copy(xw_g[:], xw[:].indirect(offs_sb[:]))
+        nc.vector.tensor_copy(xs_g[:], xs[:].indirect(offs_sb[:]))
+
+        def deal(raw, name, v_share):
+            dealt = keep.tile([P, PACK * H], BF16, name=name, align_bytes=64)
+            dst = dealt[:].rearrange("p (t m j) -> p m t j", t=PACK, j=PACK)
+            src = raw[:].rearrange("p j (m t) -> p m t j", t=PACK)
+            nc.vector.tensor_copy(dst[:, :v_share], src[:, :v_share])
+            if v_share < P:
+                nc.scalar.activation(dst[:, v_share:], src[:, v_share:], ACT.Copy)
+            return dealt
+
+        def product(dealt, name):
+            codes = keep.tile([P, H], U32, name=name + "_codes", align_bytes=64)
+            scales = keep.tile([P, H], U8, name=name + "_scales", align_bytes=64)
+            banks = []
+            for a, b in ((0, 1), (1, PACK)):
+                nc.vector.quantize_mx(out=codes[:, a * P : b * P].bitcast(FP8X4), scales=scales[:, a * P : b * P], in_=dealt[:, a * H : b * H])
+                for t in range(a, b):
+                    bank = psum.tile([P, S], F32, name=name)
+                    nc.tensor.matmul_mx(out=bank[:], lhsT=codes[:, t * P : (t + 1) * P].bitcast(FP8X4), lhsT_scale=scales[:, t * P : (t + 1) * P],
+                                        rhs=xw_g[:].bitcast(FP8X4), rhs_scale=xs_g[:], start=True, stop=True)
+                    banks.append(bank)
+            return banks
+
+        y = product(deal(w1_raw, "w1_bf", V_SHARE), "y")
+        th = [keep.tile([P, S], F32, name="th%d" % t) for t in range(PACK)]
+        for t in range(PACK):
+            nc.scalar.activation(th[t][:], y[t][:], ACT.Tanh)
+
+        du = product(deal(w2_raw, "w2_bf", P), "du")
+
+        m2u = keep.tile([P, PACK], F32, name="m2u")
+        nc.gpsimd.tensor_scalar(m2u[:], unit_sb[:], -2.0, 0.0, ALU.mult, ALU.add)
+
+        rw = [keep.tile([P, 2 * S], F32, name="rw%d" % t) for t in range(PACK)]
+        sw = [keep.tile([P, 2 * S], F32, name="sw%d" % t) for t in range(PACK)]
+        rg = [keep.tile([P, S], F32, name="rg%d" % t) for t in range(SCALAR_FETCH)]
+
+        def recip(t):
+            adu = keep.tile([P, S], F32, name="adu%d" % t)
+            nc.scalar.activation(adu[:], du[t][:], ACT.Abs)
+            nc.scalar.activation(rw[t][:, S:], adu[:], ACT.Abs_reciprocal_sqrt, bias=0.4)
+            nc.scalar.activation(rw[t][:, :S], rw[t][:, S:], ACT.Square)
+
+        recip(0)
+        for t in range(1, PACK):
+            recip(t)
+            if t - 1 < SCALAR_FETCH:
+                nc.scalar.activation(rg[t - 1][:], rw[t - 1][:].indirect(blk_sb[:]), ACT.Copy)
+
+        def enter(ts):
+            nrc = {t: keep.tile([P, S], F32, name="nrc%d" % t) for t in ts}
+            m2 = {t: keep.tile([P, S // 2], F32, name="m2%d" % t) for t in ts}
+            nb = {t: keep.tile([P, S // 4], F32, name="nb%d" % t) for t in ts}
+            e = {t: keep.tile([P, S], F32, name="e%d" % t) for t in ts}
+            for t in ts:
+                nc.vector.tensor_tensor(nrc[t][:], th[t][:], cost_sb[t][:], ALU.subtract)
+            for t in ts:
+                g = nrc[t][:].rearrange("p (v d) -> p v d", d=D)
+                nc.vector.tensor_tensor(m2[t][:].rearrange("p (v d) -> p v d", d=2), g[:, :, 0:2], g[:, :, 2:4], ALU.max)
+            for t in ts:
+                g = m2[t][:].rearrange("p (v d) -> p v d", d=2)
+                nc.vector.tensor_tensor(nb[t][:], g[:, :, 0], g[:, :, 1], ALU.max)
+            for t in ts:
+                nc.vector.tensor_tensor(e[t][:].rearrange("p (v d) -> p v d", d=D), nrc[t][:].rearrange("p (v d) -> p v d", d=D),
+                                        nb[t][:].unsqueeze(2).to_broadcast([P, S // D, D]), ALU.add)
+            for t in ts:
+                if t < SCALAR_FETCH and False:
+                    pass
+                else:
+                    nc.vector.tensor_scalar(sw[t][:, S:], e[t][:], 0.0, unit_sb[:, t : t + 1], ALU.max, ALU.mult)
+
+        enter((0, 1))
+        enter((2, 3))
+
+        w3_bf = keep.tile([P, N, PACK], BF16, name="w3_bf", align_bytes=64)
+        nc.vector.tensor_copy(w3_bf[:].rearrange("p (c i) j -> p c j i", i=4), w3_raw[:].rearrange("p j (c i) -> p c j i", i=4))
+        w3_codes = keep.tile([P, N], U32, name="w3_codes", align_bytes=64)
+        w3_scales = keep.tile([P, N], U8, name="w3_scales", align_bytes=64)
+        nc.vector.quantize_mx(out=w3_codes[:].bitcast(FP8X4), scales=w3_scales[:], in_=w3_bf[:].rearrange("p n j -> p (n j)"))
+
+        hid = keep.tile([P, PACK, S], F32, name="hid")
+        c = [keep.tile([P, S], F32, name="c%d" % t) for t in range(PACK)]
+        sg = [keep.tile([P, S], F32, name="sg%d" % t) for t in range(PACK)]
+        for t in range(PACK):
+            if t < SCALAR_FETCH:
+                nc.vector.tensor_tensor(sw[t][:, :S], rg[t][:], sw[t][:, S:], ALU.mult)
+            else:
+                nc.vector.tensor_tensor(sw[t][:, :S], rw[t][:].indirect(blk_sb[:]), sw[t][:, S:], ALU.mult)
+            nc.vector.scalar_tensor_tensor(c[t][:], du[t][:], m2u[:, t : t + 1], sw[t][:, :S], ALU.mult, ALU.add)
+        for t in range(PACK):
+            pieces = 2 if t == PACK - 1 else 1
+            w = S // pieces
+            for h in range(pieces):
+                cols = slice(h * w, (h + 1) * w)
+                nc.scalar.activation(sg[t][:, cols], sw[t][:].indirect(blk_sb[:, h * w // 16 : (h + 1) * w // 16]), ACT.Copy)
+                nc.vector.scalar_tensor_tensor(hid[:, t, cols], c[t][:, cols], -0.5, sg[t][:, cols], ALU.mult, ALU.add)
+
+        for h in range(2):
+            cols = slice(h * HALF, (h + 1) * HALF)
+            hid_bf = keep.tile([P, HALF, PACK], BF16, name="hid_bf%d" % h, align_bytes=64)
+            nc.vector.tensor_copy(hid_bf[:].rearrange("p (c i) t -> p c t i", i=4), hid[:, :, cols].rearrange("p t (c i) -> p c t i", i=4))
+            codes = keep.tile([P, HALF], U32, name="hid_codes%d" % h, align_bytes=64)
+            scales = keep.tile([P, HALF], U8, name="hid_scales%d" % h, align_bytes=64)
+            nc.vector.quantize_mx(out=codes[:].bitcast(FP8X4), scales=scales[:], in_=hid_bf[:].rearrange("p s t -> p (s t)"))
+            bank = psum.tile([P, HALF], F32, name="y")
+            nc.tensor.matmul_mx(out=bank[:], lhsT=w3_codes[:].bitcast(FP8X4), lhsT_scale=w3_scales[:],
+                                rhs=codes[:].bitcast(FP8X4), rhs_scale=scales[:], start=True, stop=True)
+            res = keep.tile([P, HALF], F32, name="res%d" % h)
+            nc.scalar.activation(res[:], bank[:], ACT.Copy)
+            nc.sync.dma_start(out[:, cols], res[:])

@@ -18,8 +18,9 @@ ACT = mybir.ActivationFunctionType
 P = 128
 PACK = 4
 V_SHARE = 80
-HALF = S // 2
-SCALAR_FETCH = 2
+CHUNKS = ((0, 256), (256, 512))
+S_PART = 32
+VECTOR_FETCH = 2
 
 
 def tile_picked_ybender_dual_p_kernel(tc, x_words, x_scales, w1, w2, cost, unit, w3, offs, blk, out):
@@ -33,9 +34,9 @@ def tile_picked_ybender_dual_p_kernel(tc, x_words, x_scales, w1, w2, cost, unit,
         xw = keep.tile([P, T], U32, name="xw")
         xs = keep.tile([P, T], U8, name="xs")
         w1_raw = keep.tile([P, PACK, H], F32, name="w1_raw")
-        w2_raw = keep.tile([P, PACK, H], F32, name="w2_raw")
+        w2_raw = [keep.tile([P, 2, H], F32, name="w2_raw%d" % a) for a in range(2)]
         w3_raw = keep.tile([P, PACK, N], F32, name="w3_raw")
-        cost_sb = [keep.tile([P, S], F32, name="cost%d" % t) for t in range(PACK)]
+        cost_sb = [keep.tile([P, 2, S], F32, name="cost%d" % a) for a in range(2)]
         unit_sb = keep.tile([P, PACK], F32, name="unit_sb")
 
         nc.gpsimd.memset(xs[:].bitcast(I32), 0)
@@ -44,27 +45,20 @@ def tile_picked_ybender_dual_p_kernel(tc, x_words, x_scales, w1, w2, cost, unit,
         for q in range(4):
             nc.sync.dma_start(xs[32 * q : 32 * q + 4, :].bitcast(I32), x_scales[0, 4 * q : 4 * q + 4, :].bitcast(I32))
         nc.sync.dma_start(w1_raw[:], w1.rearrange("(p j) c -> p j c", j=PACK))
-        nc.sync.dma_start(w2_raw[:], w2.rearrange("(p j) c -> p j c", j=PACK))
+        w2_v = w2.rearrange("(p j) c -> p j c", j=PACK)
         cost_v = cost.rearrange("(p t) s -> p t s", t=PACK)
-        nc.sync.dma_start(unit_sb[:], unit.rearrange("(p t) o -> p (t o)", t=PACK))
-        for t in range(PACK):
-            nc.sync.dma_start(cost_sb[t][:], cost_v[:, t, :])
+        for a in range(2):
+            nc.sync.dma_start(w2_raw[a][:], w2_v[:, 2 * a : 2 * a + 2, :])
+        for a in range(2):
+            nc.sync.dma_start(cost_sb[a][:], cost_v[:, 2 * a : 2 * a + 2, :])
         nc.sync.dma_start(blk_sb[:], blk)
+        nc.sync.dma_start(unit_sb[:], unit.rearrange("(p t) o -> p (t o)", t=PACK))
         nc.sync.dma_start(w3_raw[:], w3.rearrange("(p j) c -> p j c", j=PACK))
 
         xw_g = keep.tile([P, S], U32, name="xw_g", align_bytes=64)
         xs_g = keep.tile([P, S], U8, name="xs_g", align_bytes=64)
         nc.vector.tensor_copy(xw_g[:], xw[:].indirect(offs_sb[:]))
         nc.vector.tensor_copy(xs_g[:], xs[:].indirect(offs_sb[:]))
-
-        def deal(raw, name, v_share):
-            dealt = keep.tile([P, PACK * H], BF16, name=name, align_bytes=64)
-            dst = dealt[:].rearrange("p (t m j) -> p m t j", t=PACK, j=PACK)
-            src = raw[:].rearrange("p j (m t) -> p m t j", t=PACK)
-            nc.vector.tensor_copy(dst[:, :v_share], src[:, :v_share])
-            if v_share < P:
-                nc.scalar.activation(dst[:, v_share:], src[:, v_share:], ACT.Copy)
-            return dealt
 
         def product(dealt, name):
             codes = keep.tile([P, H], U32, name=name + "_codes", align_bytes=64)
@@ -79,90 +73,132 @@ def tile_picked_ybender_dual_p_kernel(tc, x_words, x_scales, w1, w2, cost, unit,
                     banks.append(bank)
             return banks
 
-        y = product(deal(w1_raw, "w1_bf", V_SHARE), "y")
-        th = [keep.tile([P, S], F32, name="th%d" % t) for t in range(PACK)]
+        w1_bf = keep.tile([P, PACK * H], BF16, name="w1_bf", tag="dealt", align_bytes=64)
+        dst = w1_bf[:].rearrange("p (t m j) -> p m j t", t=PACK, j=PACK)
+        src = w1_raw[:].rearrange("p j (m t) -> p m j t", t=PACK)
+        nc.vector.tensor_copy(dst[:, :V_SHARE], src[:, :V_SHARE])
+        nc.scalar.activation(dst[:, V_SHARE:], src[:, V_SHARE:], ACT.Copy)
+        y = product(w1_bf, "y")
+        th = [keep.tile([P, 2, S], F32, name="th%d" % a, align_bytes=64) for a in range(2)]
         for t in range(PACK):
-            nc.scalar.activation(th[t][:], y[t][:], ACT.Tanh)
+            nc.scalar.activation(th[t // 2][:, t % 2, :], y[t][:], ACT.Tanh)
 
-        du = product(deal(w2_raw, "w2_bf", P), "du")
+        w2_bf = keep.tile([P, PACK * H], BF16, name="w2_bf", tag="dealt", align_bytes=64)
+        dst = w2_bf[:].rearrange("p (t m j) -> p m j t", t=PACK, j=PACK)
+        for a in range(2):
+            nc.vector.tensor_copy(dst[:, :, 2 * a : 2 * a + 2, :], w2_raw[a][:].rearrange("p j (m t) -> p m j t", t=PACK))
+        du = product(w2_bf, "du")
 
         m2u = keep.tile([P, PACK], F32, name="m2u")
         nc.gpsimd.tensor_scalar(m2u[:], unit_sb[:], -2.0, 0.0, ALU.mult, ALU.add)
 
         rw = [keep.tile([P, 2 * S], F32, name="rw%d" % t) for t in range(PACK)]
         sw = [keep.tile([P, 2 * S], F32, name="sw%d" % t) for t in range(PACK)]
-        rg = [keep.tile([P, S], F32, name="rg%d" % t) for t in range(SCALAR_FETCH)]
+        rg = {t: keep.tile([P, S], F32, name="rg%d" % t) for t in range(VECTOR_FETCH, PACK)}
 
-        def recip(t):
-            adu = keep.tile([P, S], F32, name="adu%d" % t)
-            nc.scalar.activation(adu[:], du[t][:], ACT.Abs)
-            nc.scalar.activation(rw[t][:, S:], adu[:], ACT.Abs_reciprocal_sqrt, bias=0.4)
-            nc.scalar.activation(rw[t][:, :S], rw[t][:, S:], ACT.Square)
+        adu = [rw[t][:, S:] if t >= VECTOR_FETCH else keep.tile([P, S], F32, name="adu%d" % t)[:] for t in range(PACK)]
+        rs = [rw[t][:, :S] if t >= VECTOR_FETCH else rw[t][:, S:] for t in range(PACK)]
+        for t in range(PACK):
+            nc.scalar.activation(adu[t], du[t][:], ACT.Abs)
 
-        recip(0)
-        for t in range(1, PACK):
-            recip(t)
-            if t - 1 < SCALAR_FETCH:
-                nc.scalar.activation(rg[t - 1][:], rw[t - 1][:].indirect(blk_sb[:]), ACT.Copy)
+        def finish_recip(t):
+            if t >= VECTOR_FETCH:
+                nc.scalar.activation(rg[t][:], rw[t][:].indirect(blk_sb[:]), ACT.Copy)
+            else:
+                nc.scalar.activation(rw[t][:, :S], rs[t], ACT.Square)
 
-        def enter(ts):
-            nrc = {t: keep.tile([P, S], F32, name="nrc%d" % t) for t in ts}
-            m2 = {t: keep.tile([P, S // 2], F32, name="m2%d" % t) for t in ts}
-            nb = {t: keep.tile([P, S // 4], F32, name="nb%d" % t) for t in ts}
-            e = {t: keep.tile([P, S], F32, name="e%d" % t) for t in ts}
-            for t in ts:
-                nc.vector.tensor_tensor(nrc[t][:], th[t][:], cost_sb[t][:], ALU.subtract)
-            for t in ts:
-                g = nrc[t][:].rearrange("p (v d) -> p v d", d=D)
-                nc.vector.tensor_tensor(m2[t][:].rearrange("p (v d) -> p v d", d=2), g[:, :, 0:2], g[:, :, 2:4], ALU.max)
-            for t in ts:
-                g = m2[t][:].rearrange("p (v d) -> p v d", d=2)
-                nc.vector.tensor_tensor(nb[t][:], g[:, :, 0], g[:, :, 1], ALU.max)
-            for t in ts:
-                nc.vector.tensor_tensor(e[t][:].rearrange("p (v d) -> p v d", d=D), nrc[t][:].rearrange("p (v d) -> p v d", d=D),
-                                        nb[t][:].unsqueeze(2).to_broadcast([P, S // D, D]), ALU.add)
-            for t in ts:
-                if t < SCALAR_FETCH and False:
-                    pass
-                else:
-                    nc.vector.tensor_scalar(sw[t][:, S:], e[t][:], 0.0, unit_sb[:, t : t + 1], ALU.max, ALU.mult)
+        for t in range(PACK):
+            nc.scalar.activation(rs[t], adu[t], ACT.Abs_reciprocal_sqrt, bias=0.4)
+            if t > 0:
+                finish_recip(t - 1)
+        finish_recip(PACK - 1)
 
-        enter((0, 1))
-        enter((2, 3))
+        nrc = [keep.tile([P, 2 * S], F32, name="nrc0", tag="dealt", align_bytes=64), keep.tile([P, 2 * S], F32, name="nrc1", tag="w2_raw1")]
+        m2 = [keep.tile([P, S], F32, name="m2%d" % a) for a in range(2)]
+        nb = [keep.tile([P, S // 2], F32, name="nb%d" % a) for a in range(2)]
+        e = [keep.tile([P, 2 * S], F32, name="e%d" % a) for a in range(2)]
+        for a in range(2):
+            nc.vector.tensor_tensor(nrc[a][:], th[a][:].rearrange("p t s -> p (t s)"), cost_sb[a][:].rearrange("p t s -> p (t s)"), ALU.subtract)
+        for a in range(2):
+            g = nrc[a][:].rearrange("p (v d) -> p v d", d=D)
+            nc.vector.tensor_tensor(m2[a][:].rearrange("p (v d) -> p v d", d=2), g[:, :, 0:2], g[:, :, 2:4], ALU.max)
+        for a in range(2):
+            g = m2[a][:].rearrange("p (v d) -> p v d", d=2)
+            nc.vector.tensor_tensor(nb[a][:], g[:, :, 0], g[:, :, 1], ALU.max)
+        for a in range(2):
+            nc.vector.tensor_tensor(e[a][:].rearrange("p (v d) -> p v d", d=D), nrc[a][:].rearrange("p (v d) -> p v d", d=D),
+                                    nb[a][:].unsqueeze(2).to_broadcast([P, 2 * S // D, D]), ALU.add)
 
-        w3_bf = keep.tile([P, N, PACK], BF16, name="w3_bf", align_bytes=64)
+        w3_bf = keep.tile([P, N, PACK], BF16, name="w3_bf", tag="th1", align_bytes=64)
         nc.vector.tensor_copy(w3_bf[:].rearrange("p (c i) j -> p c j i", i=4), w3_raw[:].rearrange("p j (c i) -> p c j i", i=4))
         w3_codes = keep.tile([P, N], U32, name="w3_codes", align_bytes=64)
         w3_scales = keep.tile([P, N], U8, name="w3_scales", align_bytes=64)
-        nc.vector.quantize_mx(out=w3_codes[:].bitcast(FP8X4), scales=w3_scales[:], in_=w3_bf[:].rearrange("p n j -> p (n j)"))
 
         hid = keep.tile([P, PACK, S], F32, name="hid")
         c = [keep.tile([P, S], F32, name="c%d" % t) for t in range(PACK)]
         sg = [keep.tile([P, S], F32, name="sg%d" % t) for t in range(PACK)]
-        for t in range(PACK):
-            if t < SCALAR_FETCH:
-                nc.vector.tensor_tensor(sw[t][:, :S], rg[t][:], sw[t][:, S:], ALU.mult)
+
+        def first(t):
+            e_t = e[t // 2][:, (t % 2) * S : (t % 2 + 1) * S]
+            if t >= VECTOR_FETCH:
+                nc.vector.scalar_tensor_tensor(sw[t][:, S:], e_t, 0.0, rg[t][:], ALU.max, ALU.mult)
+            else:
+                nc.vector.tensor_scalar(sw[t][:, S:], e_t, 0.0, unit_sb[:, t : t + 1], ALU.max, ALU.mult)
+
+        def second(t):
+            if t >= VECTOR_FETCH:
+                nc.vector.scalar_tensor_tensor(sw[t][:, :S], sw[t][:, S:], unit_sb[:, t : t + 1], rg[t][:], ALU.mult, ALU.mult)
             else:
                 nc.vector.tensor_tensor(sw[t][:, :S], rw[t][:].indirect(blk_sb[:]), sw[t][:, S:], ALU.mult)
+
+        def third(t):
             nc.vector.scalar_tensor_tensor(c[t][:], du[t][:], m2u[:, t : t + 1], sw[t][:, :S], ALU.mult, ALU.add)
-        for t in range(PACK):
-            pieces = 2 if t == PACK - 1 else 1
-            w = S // pieces
-            for h in range(pieces):
-                cols = slice(h * w, (h + 1) * w)
-                nc.scalar.activation(sg[t][:, cols], sw[t][:].indirect(blk_sb[:, h * w // 16 : (h + 1) * w // 16]), ACT.Copy)
+
+        def fourth(t):
+            for a, b in CHUNKS if t == PACK - 1 else ((0, S),):
+                cols = slice(a, b)
+                nc.scalar.activation(sg[t][:, cols], sw[t][:].indirect(blk_sb[:, a // 16 : b // 16]), ACT.Copy)
                 nc.vector.scalar_tensor_tensor(hid[:, t, cols], c[t][:, cols], -0.5, sg[t][:, cols], ALU.mult, ALU.add)
 
-        for h in range(2):
-            cols = slice(h * HALF, (h + 1) * HALF)
-            hid_bf = keep.tile([P, HALF, PACK], BF16, name="hid_bf%d" % h, align_bytes=64)
-            nc.vector.tensor_copy(hid_bf[:].rearrange("p (c i) t -> p c t i", i=4), hid[:, :, cols].rearrange("p t (c i) -> p c t i", i=4))
-            codes = keep.tile([P, HALF], U32, name="hid_codes%d" % h, align_bytes=64)
-            scales = keep.tile([P, HALF], U8, name="hid_scales%d" % h, align_bytes=64)
-            nc.vector.quantize_mx(out=codes[:].bitcast(FP8X4), scales=scales[:], in_=hid_bf[:].rearrange("p s t -> p (s t)"))
-            bank = psum.tile([P, HALF], F32, name="y")
+        first(0)
+        nc.vector.quantize_mx(out=w3_codes[:].bitcast(FP8X4), scales=w3_scales[:], in_=w3_bf[:].rearrange("p n j -> p (n j)"))
+        for t in range(PACK):
+            second(t)
+            if t + 1 < PACK:
+                first(t + 1)
+            else:
+                fourth(0)
+            third(t)
+        for t in range(1, PACK):
+            fourth(t)
+
+        hid_bf = [keep.tile([P, b - a, PACK], BF16, name="hid_bf%d" % a, align_bytes=64) for a, b in CHUNKS]
+
+        def weave(h):
+            a, b = CHUNKS[h]
+            dst = hid_bf[h][:].rearrange("p (c i) t -> p c t i", i=4)
+            src = hid[:, :, a:b].rearrange("p t (c i) -> p c t i", i=4)
+            if h == 0 and S_PART:
+                nc.scalar.activation(dst[:, :S_PART], src[:, :S_PART], ACT.Copy)
+                if S_PART < (b - a) // 4:
+                    nc.vector.tensor_copy(dst[:, S_PART:], src[:, S_PART:])
+            else:
+                nc.vector.tensor_copy(dst, src)
+
+        def last_product(h):
+            a, b = CHUNKS[h]
+            codes = keep.tile([P, b - a], U32, name="hid_codes%d" % h, align_bytes=64)
+            scales = keep.tile([P, b - a], U8, name="hid_scales%d" % h, align_bytes=64)
+            nc.vector.quantize_mx(out=codes[:].bitcast(FP8X4), scales=scales[:], in_=hid_bf[h][:].rearrange("p s t -> p (s t)"))
+            bank = psum.tile([P, b - a], F32, name="y")
             nc.tensor.matmul_mx(out=bank[:], lhsT=w3_codes[:].bitcast(FP8X4), lhsT_scale=w3_scales[:],
                                 rhs=codes[:].bitcast(FP8X4), rhs_scale=scales[:], start=True, stop=True)
-            res = keep.tile([P, HALF], F32, name="res%d" % h)
+            res = keep.tile([P, b - a], F32, name="res%d" % h)
             nc.scalar.activation(res[:], bank[:], ACT.Copy)
-            nc.sync.dma_start(out[:, cols], res[:])
+            nc.sync.dma_start(out[:, a:b], res[:])
+
+        weave(0)
+        for h in range(len(CHUNKS)):
+            if h + 1 < len(CHUNKS):
+                weave(h + 1)
+            last_product(h)

@@ -40,8 +40,8 @@ def tile_picked_ybender_dual_p_kernel(tc, x_words, x_scales, w1, w2, cost, unit,
         unit_sb = keep.tile([P, PACK], F32, name="unit_sb")
 
         nc.gpsimd.memset(xs[:].bitcast(I32), 0)
-        nc.sync.dma_start(offs_sb[:], offs)
         nc.sync.dma_start(xw[:].bitcast(I32), x_words[0].rearrange("p n t -> p (n t)").bitcast(I32))
+        nc.sync.dma_start(offs_sb[:], offs)
         for q in range(4):
             nc.sync.dma_start(xs[32 * q : 32 * q + 4, :].bitcast(I32), x_scales[0, 4 * q : 4 * q + 4, :].bitcast(I32))
         nc.sync.dma_start(w1_raw[:], w1.rearrange("(p j) c -> p j c", j=PACK))
@@ -74,8 +74,8 @@ def tile_picked_ybender_dual_p_kernel(tc, x_words, x_scales, w1, w2, cost, unit,
             return banks
 
         w1_bf = keep.tile([P, PACK * H], BF16, name="w1_bf", tag="dealt", align_bytes=64)
-        dst = w1_bf[:].rearrange("p (t m j) -> p m j t", t=PACK, j=PACK)
-        src = w1_raw[:].rearrange("p j (m t) -> p m j t", t=PACK)
+        dst = w1_bf[:].rearrange("p (t m j) -> p m t j", t=PACK, j=PACK)
+        src = w1_raw[:].rearrange("p j (m t) -> p m t j", t=PACK)
         nc.vector.tensor_copy(dst[:, :V_SHARE], src[:, :V_SHARE])
         nc.scalar.activation(dst[:, V_SHARE:], src[:, V_SHARE:], ACT.Copy)
         y = product(w1_bf, "y")
@@ -84,9 +84,9 @@ def tile_picked_ybender_dual_p_kernel(tc, x_words, x_scales, w1, w2, cost, unit,
             nc.scalar.activation(th[t // 2][:, t % 2, :], y[t][:], ACT.Tanh)
 
         w2_bf = keep.tile([P, PACK * H], BF16, name="w2_bf", tag="dealt", align_bytes=64)
-        dst = w2_bf[:].rearrange("p (t m j) -> p m j t", t=PACK, j=PACK)
+        dst = w2_bf[:].rearrange("p (t m n j) -> p m t n j", t=PACK, n=2, j=PACK)
         for a in range(2):
-            nc.vector.tensor_copy(dst[:, :, 2 * a : 2 * a + 2, :], w2_raw[a][:].rearrange("p j (m t) -> p m j t", t=PACK))
+            nc.vector.tensor_copy(dst[:, :, :, :, 2 * a : 2 * a + 2], w2_raw[a][:].rearrange("p j (m n t) -> p m t n j", n=2, t=PACK))
         du = product(w2_bf, "du")
 
         m2u = keep.tile([P, PACK], F32, name="m2u")

from contextlib import ExitStack

import concourse.mybir as mybir

K, T, S, D, N, H = 512, 2048, 512, 4, 128, 512
FLOPS = 2 * K * H * S * 2 + 2 * H * N * S

F32 = mybir.dt.float32
BF16 = mybir.dt.bfloat16
I32 = mybir.dt.int32
U32 = mybir.dt.uint32
U16 = mybir.dt.uint16
U8 = mybir.dt.uint8
FP8X4 = mybir.dt.float8_e4m3fn_x4
ALU = mybir.AluOpType
ACT = mybir.ActivationFunctionType

P = 128
PACK = 4
V_SHARE = 80
CHUNKS = ((0, 256), (256, 512))
S_PART = 32
VECTOR_FETCH = 2


def tile_picked_ybender_dual_p_kernel(tc, x_words, x_scales, w1, w2, cost, unit, w3, offs, blk, out):
    nc = tc.nc
    with ExitStack() as ctx:
        keep = ctx.enter_context(tc.tile_pool(name="keep", bufs=1))
        psum = ctx.enter_context(tc.psum_pool(name="psum", bufs=4))

        offs_sb = keep.tile([P, S // 16], U16, name="offs_sb")
        blk_sb = keep.tile([P, S // 16], U16, name="blk_sb")
        xw = keep.tile([P, T], U32, name="xw")
        xs = keep.tile([P, T], U8, name="xs")
        w1_raw = keep.tile([P, PACK, H], F32, name="w1_raw")
        w2_raw = [keep.tile([P, 2, H], F32, name="w2_raw%d" % a) for a in range(2)]
        w3_raw = keep.tile([P, PACK, N], F32, name="w3_raw")
        cost_sb = [keep.tile([P, 2, S], F32, name="cost%d" % a) for a in range(2)]
        unit_sb = keep.tile([P, PACK], F32, name="unit_sb")

        nc.gpsimd.memset(xs[:].bitcast(I32), 0)
        nc.sync.dma_start(xw[:].bitcast(I32), x_words[0].rearrange("p n t -> p (n t)").bitcast(I32))
        nc.sync.dma_start(offs_sb[:], offs)
        for q in range(4):
            nc.sync.dma_start(xs[32 * q : 32 * q + 4, :].bitcast(I32), x_scales[0, 4 * q : 4 * q + 4, :].bitcast(I32))
        nc.sync.dma_start(w1_raw[:], w1.rearrange("(p j) c -> p j c", j=PACK))
        w2_v = w2.rearrange("(p j) c -> p j c", j=PACK)
        cost_v = cost.rearrange("(p t) s -> p t s", t=PACK)
        for a in range(2):
            nc.sync.dma_start(w2_raw[a][:], w2_v[:, 2 * a : 2 * a + 2, :])
        for a in range(2):
            nc.sync.dma_start(cost_sb[a][:], cost_v[:, 2 * a : 2 * a + 2, :])
        nc.sync.dma_start(blk_sb[:], blk)
        nc.sync.dma_start(unit_sb[:], unit.rearrange("(p t) o -> p (t o)", t=PACK))
        nc.sync.dma_start(w3_raw[:], w3.rearrange("(p j) c -> p j c", j=PACK))

        xw_g = keep.tile([P, S], U32, name="xw_g", align_bytes=64)
        xs_g = keep.tile([P, S], U8, name="xs_g", align_bytes=64)
        nc.vector.tensor_copy(xw_g[:], xw[:].indirect(offs_sb[:]))
        nc.vector.tensor_copy(xs_g[:], xs[:].indirect(offs_sb[:]))

        def product(dealt, name):
            codes = keep.tile([P, H], U32, name=name + "_codes", align_bytes=64)
            scales = keep.tile([P, H], U8, name=name + "_scales", align_bytes=64)
            banks = []
            for a, b in ((0, 1), (1, PACK)):
                nc.vector.quantize_mx(out=codes[:, a * P : b * P].bitcast(FP8X4), scales=scales[:, a * P : b * P], in_=dealt[:, a * H : b * H])
                for t in range(a, b):
                    bank = psum.tile([P, S], F32, name=name)
                    nc.tensor.matmul_mx(out=bank[:], lhsT=codes[:, t * P : (t + 1) * P].bitcast(FP8X4), lhsT_scale=scales[:, t * P : (t + 1) * P],
                                        rhs=xw_g[:].bitcast(FP8X4), rhs_scale=xs_g[:], start=True, stop=True)
                    banks.append(bank)
            return banks

        w1_bf = keep.tile([P, PACK * H], BF16, name="w1_bf", tag="dealt", align_bytes=64)
        dst = w1_bf[:].rearrange("p (t m j) -> p m t j", t=PACK, j=PACK)
        src = w1_raw[:].rearrange("p j (m t) -> p m t j", t=PACK)
        nc.vector.tensor_copy(dst[:, :V_SHARE], src[:, :V_SHARE])
        nc.scalar.activation(dst[:, V_SHARE:], src[:, V_SHARE:], ACT.Copy)
        y = product(w1_bf, "y")
        th = [keep.tile([P, 2, S], F32, name="th%d" % a, align_bytes=64) for a in range(2)]
        for t in range(PACK):
            nc.scalar.activation(th[t // 2][:, t % 2, :], y[t][:], ACT.Tanh)

        w2_bf = keep.tile([P, PACK * H], BF16, name="w2_bf", tag="dealt", align_bytes=64)
        dst = w2_bf[:].rearrange("p (t m n j) -> p m t n j", t=PACK, n=2, j=PACK)
        for a in range(2):
            nc.vector.tensor_copy(dst[:, :, :, :, 2 * a : 2 * a + 2], w2_raw[a][:].rearrange("p j (m n t) -> p m t n j", n=2, t=PACK))
        du = product(w2_bf, "du")

        m2u = keep.tile([P, PACK], F32, name="m2u")
        nc.gpsimd.tensor_scalar(m2u[:], unit_sb[:], -2.0, 0.0, ALU.mult, ALU.add)

        rw = [keep.tile([P, 2 * S], F32, name="rw%d" % t) for t in range(PACK)]
        sw = [keep.tile([P, 2 * S], F32, name="sw%d" % t) for t in range(PACK)]
        rg = {t: keep.tile([P, S], F32, name="rg%d" % t) for t in range(VECTOR_FETCH, PACK)}

        adu = [rw[t][:, S:] if t >= VECTOR_FETCH else keep.tile([P, S], F32, name="adu%d" % t)[:] for t in range(PACK)]
        rs = [rw[t][:, :S] if t >= VECTOR_FETCH else rw[t][:, S:] for t in range(PACK)]
        for t in range(PACK):
            nc.scalar.activation(adu[t], du[t][:], ACT.Abs)

        def finish_recip(t):
            if t >= VECTOR_FETCH:
                nc.scalar.activation(rg[t][:], rw[t][:].indirect(blk_sb[:]), ACT.Copy)
            else:
                nc.scalar.activation(rw[t][:, :S], rs[t], ACT.Square)

        for t in range(PACK):
            nc.scalar.activation(rs[t], adu[t], ACT.Abs_reciprocal_sqrt, bias=0.4)
            if t > 0:
                finish_recip(t - 1)
        finish_recip(PACK - 1)

        nrc = [keep.tile([P, 2 * S], F32, name="nrc0", tag="dealt", align_bytes=64), keep.tile([P, 2 * S], F32, name="nrc1", tag="w2_raw1")]
        m2 = [keep.tile([P, S], F32, name="m2%d" % a) for a in range(2)]
        nb = [keep.tile([P, S // 2], F32, name="nb%d" % a) for a in range(2)]
        e = [keep.tile([P, 2 * S], F32, name="e%d" % a) for a in range(2)]
        for a in range(2):
            nc.vector.tensor_tensor(nrc[a][:], th[a][:].rearrange("p t s -> p (t s)"), cost_sb[a][:].rearrange("p t s -> p (t s)"), ALU.subtract)
        for a in range(2):
            g = nrc[a][:].rearrange("p (v d) -> p v d", d=D)
            nc.vector.tensor_tensor(m2[a][:].rearrange("p (v d) -> p v d", d=2), g[:, :, 0:2], g[:, :, 2:4], ALU.max)
        for a in range(2):
            g = m2[a][:].rearrange("p (v d) -> p v d", d=2)
            nc.vector.tensor_tensor(nb[a][:], g[:, :, 0], g[:, :, 1], ALU.max)
        for a in range(2):
            nc.vector.tensor_tensor(e[a][:].rearrange("p (v d) -> p v d", d=D), nrc[a][:].rearrange("p (v d) -> p v d", d=D),
                                    nb[a][:].unsqueeze(2).to_broadcast([P, 2 * S // D, D]), ALU.add)

        w3_bf = keep.tile([P, N, PACK], BF16, name="w3_bf", tag="th1", align_bytes=64)
        nc.vector.tensor_copy(w3_bf[:].rearrange("p (c i) j -> p c j i", i=4), w3_raw[:].rearrange("p j (c i) -> p c j i", i=4))
        w3_codes = keep.tile([P, N], U32, name="w3_codes", align_bytes=64)
        w3_scales = keep.tile([P, N], U8, name="w3_scales", align_bytes=64)

        hid = keep.tile([P, PACK, S], F32, name="hid")
        c = [keep.tile([P, S], F32, name="c%d" % t) for t in range(PACK)]
        sg = [keep.tile([P, S], F32, name="sg%d" % t) for t in range(PACK)]

        def first(t):
            e_t = e[t // 2][:, (t % 2) * S : (t % 2 + 1) * S]
            if t >= VECTOR_FETCH:
                nc.vector.scalar_tensor_tensor(sw[t][:, S:], e_t, 0.0, rg[t][:], ALU.max, ALU.mult)
            else:
                nc.vector.tensor_scalar(sw[t][:, S:], e_t, 0.0, unit_sb[:, t : t + 1], ALU.max, ALU.mult)

        def second(t):
            if t >= VECTOR_FETCH:
                nc.vector.scalar_tensor_tensor(sw[t][:, :S], sw[t][:, S:], unit_sb[:, t : t + 1], rg[t][:], ALU.mult, ALU.mult)
            else:
                nc.vector.tensor_tensor(sw[t][:, :S], rw[t][:].indirect(blk_sb[:]), sw[t][:, S:], ALU.mult)

        def third(t):
            nc.vector.scalar_tensor_tensor(c[t][:], du[t][:], m2u[:, t : t + 1], sw[t][:, :S], ALU.mult, ALU.add)

        def fourth(t):
            for a, b in CHUNKS if t == PACK - 1 else ((0, S),):
                cols = slice(a, b)
                nc.scalar.activation(sg[t][:, cols], sw[t][:].indirect(blk_sb[:, a // 16 : b // 16]), ACT.Copy)
                nc.vector.scalar_tensor_tensor(hid[:, t, cols], c[t][:, cols], -0.5, sg[t][:, cols], ALU.mult, ALU.add)

        first(0)
        nc.vector.quantize_mx(out=w3_codes[:].bitcast(FP8X4), scales=w3_scales[:], in_=w3_bf[:].rearrange("p n j -> p (n j)"))
        for t in range(PACK):
            second(t)
            if t + 1 < PACK:
                first(t + 1)
            else:
                fourth(0)
            third(t)
        for t in range(1, PACK):
            fourth(t)

        hid_bf = [keep.tile([P, b - a, PACK], BF16, name="hid_bf%d" % a, align_bytes=64) for a, b in CHUNKS]

        def weave(h):
            a, b = CHUNKS[h]
            dst = hid_bf[h][:].rearrange("p (c i) t -> p c t i", i=4)
            src = hid[:, :, a:b].rearrange("p t (c i) -> p c t i", i=4)
            if h == 0 and S_PART:
                nc.scalar.activation(dst[:, :S_PART], src[:, :S_PART], ACT.Copy)
                if S_PART < (b - a) // 4:
                    nc.vector.tensor_copy(dst[:, S_PART:], src[:, S_PART:])
            else:
                nc.vector.tensor_copy(dst, src)

        def last_product(h):
            a, b = CHUNKS[h]
            codes = keep.tile([P, b - a], U32, name="hid_codes%d" % h, align_bytes=64)
            scales = keep.tile([P, b - a], U8, name="hid_scales%d" % h, align_bytes=64)
            nc.vector.quantize_mx(out=codes[:].bitcast(FP8X4), scales=scales[:], in_=hid_bf[h][:].rearrange("p s t -> p (s t)"))
            bank = psum.tile([P, b - a], F32, name="y")
            nc.tensor.matmul_mx(out=bank[:], lhsT=w3_codes[:].bitcast(FP8X4), lhsT_scale=w3_scales[:],
                                rhs=codes[:].bitcast(FP8X4), rhs_scale=scales[:], start=True, stop=True)
            res = keep.tile([P, b - a], F32, name="res%d" % h)
            nc.scalar.activation(res[:], bank[:], ACT.Copy)
            nc.sync.dma_start(out[:, a:b], res[:])

        weave(0)
        for h in range(len(CHUNKS)):
            if h + 1 < len(CHUNKS):
                weave(h + 1)
            last_product(h)
